import numpy as np
import ml_dtypes


def mxq(x, axis, fmt="e4m3"):
    dtype, down = {"e4m3": (ml_dtypes.float8_e4m3fn, 7), "e5m2": (ml_dtypes.float8_e5m2, 14)}[fmt]
    v = np.moveaxis(np.asarray(x, np.float32).astype(ml_dtypes.bfloat16).astype(np.float64), axis, -1)
    blocks = v.reshape(v.shape[:-1] + (-1, 32))
    amax = np.abs(blocks).max(-1, keepdims=True)
    byte = np.maximum(np.where(amax > 0, np.frexp(amax)[1] - 1 + 127, 0) - down, 1)
    scale = np.exp2(byte - 127.0)
    codes = (blocks / scale).astype(np.float32).astype(dtype).astype(np.float64)
    return np.moveaxis((codes * scale).reshape(v.shape), -1, axis)


WIDE = False


def mx_kscale(k):
    if not WIDE:
        return np.ones(k)
    levels = np.array([10, -10, 5, -5, 0])
    if k % 512:
        return np.exp2(np.random.permutation(np.resize(levels, k // 32))).repeat(32)
    a = np.empty((k // 512, 16))
    for p in range(k // 512):
        a[p, :8] = np.random.permutation(np.resize(levels, 8))
        for g in range(8):
            far = levels[np.abs(levels - a[p, g]) >= 10]
            a[p, g + 8] = far[np.random.randint(len(far))]
    return np.exp2(a.ravel()).repeat(32)


def f64(x):
    return np.asarray(x).astype(np.float64)


def striped(idx):
    return np.tile(idx.reshape(-1, 16).T, (8, 1)).astype(np.uint16)


def unstriped(offs):
    return offs[:16].T.reshape(-1).astype(np.int64)


def silu(v):
    return v / (1.0 + np.exp(-np.maximum(v, -700.0)))


K, T, H, N = 512, 128, 512, 512


def setup_inputs():
    n = np.random.standard_normal
    s = mx_kscale(K)[:, None]
    u = mx_kscale(H)
    idx = np.random.permutation(H)
    v = np.empty(H)
    v[idx] = u
    return {
        "xT": (n((K, T)) * s).astype(np.float32),
        "w1": (n((K, H)) / np.sqrt(K) / s * v).astype(np.float32),
        "w2": (n((H, N)) / np.sqrt(H) / u[:, None]).astype(np.float32),
        "offs": striped(idx),
    }


def reference(xT, w1, w2, offs):
    idx = unstriped(offs)
    h = silu(mxq(f64(w1), 0, "e4m3").T @ mxq(f64(xT), 0, "e4m3"))
    return mxq(f64(w2), 0, "e4m3").T @ mxq(h[idx], 0, "e4m3")

@@ -1,0 +1,155 @@
+from contextlib import ExitStack
+
+import concourse.mybir as mybir
+from concourse.masks import make_identity
+
+K, T, H, N = 512, 128, 512, 512
+FLOPS = 2 * T * H * (K + N)
+
+F32 = mybir.dt.float32
+BF16 = mybir.dt.bfloat16
+U32 = mybir.dt.uint32
+U16 = mybir.dt.uint16
+U8 = mybir.dt.uint8
+FP8X4 = mybir.dt.float8_e4m3fn_x4
+SILU = mybir.ActivationFunctionType.Silu
+COPY = mybir.ActivationFunctionType.Copy
+
+P = 128
+PACK = 4
+
+W1_PIECES = (256, 128, 128)
+W1_VECTOR = (176, 88, 88)
+W2_PIECES = (256, 256)
+W2_VECTOR = (160, 160)
+V_GATHER = 320
+
+
+def tile_picked_shuffle_mlp_silu_perm_l_kernel(tc, xT, w1, w2, offs, out):
+    nc = tc.nc
+    with ExitStack() as ctx:
+        keep = ctx.enter_context(tc.tile_pool(name="keep", bufs=1))
+        psum = ctx.enter_context(tc.psum_pool(name="psum", bufs=1))
+
+        offsets = keep.tile([P, H // 16], U16, name="offsets")
+        x_raw = keep.tile([P, PACK, T], F32, name="x_raw")
+        nc.sync.dma_start(x_raw[:], xT.rearrange("(p j) t -> p j t", j=PACK))
+        w1_raw = []
+        c0 = 0
+        for i, width in enumerate(W1_PIECES):
+            raw = keep.tile([P, PACK, width], F32, name=f"w1_raw{i}")
+            nc.sync.dma_start(raw[:], w1[:, c0 : c0 + width].rearrange("(p j) w -> p j w", j=PACK))
+            w1_raw.append(raw)
+            c0 += width
+        nc.sync.dma_start(offsets[:], offs)
+        w2_raw = []
+        c0 = 0
+        for i, width in enumerate(W2_PIECES):
+            raw = keep.tile([P, PACK, width], F32, name=f"w2_raw{i}")
+            nc.sync.dma_start(raw[:], w2[:, c0 : c0 + width].rearrange("(p j) w -> p j w", j=PACK))
+            w2_raw.append(raw)
+            c0 += width
+
+        warm = keep.tile([P, 1], F32, name="warm")
+        nc.vector.memset(warm[:], 0.0)
+        nc.scalar.activation(warm[:], warm[:], SILU)
+        ident = keep.tile([P, P], F32, name="ident")
+        make_identity(nc, ident[:])
+
+        def quantize(grouped, codes, scales):
+            nc.vector.quantize_mx(
+                out=codes.bitcast(FP8X4), scales=scales, in_=grouped.rearrange("p w j -> p (w j)")
+            )
+
+        def interleave(raw, grouped, width, vector_share):
+            src = raw[:].rearrange("p j w -> p w j")
+            if vector_share > 0:
+                nc.vector.tensor_copy(out=grouped[:, 0:vector_share, :], in_=src[:, 0:vector_share, :])
+            if vector_share < width:
+                nc.scalar.copy(out=grouped[:, vector_share:width, :], in_=src[:, vector_share:width, :])
+
+        x_grouped = keep.tile([P, T, PACK], BF16, name="x_grouped", align_bytes=64)
+        x_codes = keep.tile([P, T], U32, name="x_codes", align_bytes=64)
+        x_scales = keep.tile([P, T], U8, name="x_scales", align_bytes=64)
+        interleave(x_raw, x_grouped, T, T)
+        quantize(x_grouped[:], x_codes[:], x_scales[:])
+
+        w1_codes = keep.tile([P, H], U32, name="w1_codes", align_bytes=64)
+        w1_scales = keep.tile([P, H], U8, name="w1_scales", align_bytes=64)
+        h = keep.tile([P, H], F32, name="h", align_bytes=64)
+        h16 = keep.tile([P, H], BF16, name="h16", align_bytes=64)
+        c0 = 0
+        for i, width in enumerate(W1_PIECES):
+            cols = slice(c0, c0 + width)
+            grouped = keep.tile([P, width, PACK], BF16, name=f"w1_grouped{i}", align_bytes=64)
+            interleave(w1_raw[i], grouped, width, W1_VECTOR[i])
+            quantize(grouped[:], w1_codes[:, cols], w1_scales[:, cols])
+            acc = psum.tile([P, width], F32, name=f"acc{i}")
+            nc.tensor.matmul_mx(
+                out=acc[:],
+                lhsT=x_codes[:].bitcast(FP8X4),
+                lhsT_scale=x_scales[:],
+                rhs=w1_codes[:, cols].bitcast(FP8X4),
+                rhs_scale=w1_scales[:, cols],
+                start=True,
+                stop=True,
+            )
+            nc.scalar.activation(h[:, cols], acc[:], SILU)
+            if V_GATHER < H:
+                nc.scalar.activation(h16[:, cols], acc[:], SILU)
+            c0 += width
+
+        picked = keep.tile([P, H], BF16, name="picked", align_bytes=64)
+        ordered = picked[:].rearrange("q (u p e) -> q p u e", u=2, e=2)
+        nc.vector.tensor_copy(
+            ordered[:, 0 : V_GATHER // PACK], h[:].indirect(offsets[:, 0 : V_GATHER // 16])
+        )
+        if V_GATHER < H:
+            nc.scalar.activation(
+                ordered[:, V_GATHER // PACK : P], h16[:].indirect(offsets[:, V_GATHER // 16 : H // 16]), COPY
+            )
+
+        w2_codes = keep.tile([P, N], U32, name="w2_codes", align_bytes=64)
+        w2_scales = keep.tile([P, N], U8, name="w2_scales", align_bytes=64)
+        c0 = 0
+        for i, width in enumerate(W2_PIECES):
+            cols = slice(c0, c0 + width)
+            grouped = keep.tile([P, width, PACK], BF16, name=f"w2_grouped{i}", align_bytes=64)
+            interleave(w2_raw[i], grouped, width, W2_VECTOR[i])
+            quantize(grouped[:], w2_codes[:, cols], w2_scales[:, cols])
+            c0 += width
+
+        turned = psum.tile([P, 2, T], F32, name="turned")
+        words = picked[:].bitcast(F32)
+        for u in range(2):
+            nc.tensor.transpose(turned[:, u, :], words[:, u * P : (u + 1) * P], ident[:])
+        h_grouped = keep.tile([P, T, PACK], BF16, name="h_grouped", align_bytes=64)
+        nc.scalar.copy(
+            out=h_grouped[:].rearrange("p t j -> p (t j)").bitcast(F32).rearrange("p (t u) -> p t u", u=2),
+            in_=turned[:].rearrange("p u t -> p t u"),
+        )
+        h_codes = keep.tile([P, T], U32, name="h_codes", align_bytes=64)
+        h_scales = keep.tile([P, T], U8, name="h_scales", align_bytes=64)
+        quantize(h_grouped[:], h_codes[:], h_scales[:])
+
+        for half in range(2):
+            acc2 = psum.tile([P, 2, T], F32, name=f"acc2_{half}")
+            for b in range(2):
+                m = slice((2 * half + b) * P, (2 * half + b + 1) * P)
+                nc.tensor.matmul_mx(
+                    out=acc2[:, b, :],
+                    lhsT=w2_codes[:, m].bitcast(FP8X4),
+                    lhsT_scale=w2_scales[:, m],
+                    rhs=h_codes[:].bitcast(FP8X4),
+                    rhs_scale=h_scales[:],
+                    start=True,
+                    stop=True,
+                )
+            result = keep.tile([P, 2, T], F32, name=f"result{half}")
+            rows = out[2 * P * half : 2 * P * (half + 1), :].rearrange("(b p) t -> p b t", p=P)
+            if half == 0:
+                nc.vector.tensor_copy(out=result[:], in_=acc2[:])
+                nc.sync.dma_start(rows, result[:])
+            else:
+                nc.scalar.copy(out=result[:], in_=acc2[:])
+                nc.scalar.dma_start(rows, result[:])

@@ -18,11 +18,11 @@ COPY = mybir.ActivationFunctionType.Copy
 P = 128
 PACK = 4
 
-W1_PIECES = (256, 128, 128)
-W1_VECTOR = (176, 88, 88)
-W2_PIECES = (256, 256)
-W2_VECTOR = (160, 160)
-V_GATHER = 320
+W1_LOADS = (320, 192)
+W1_CHUNKS = ((0, 256, (("v", 176), ("s", 80))), (256, 64, (("v", 44), ("s", 20))), (320, 128, (("v", 80), ("s", 48))), (448, 64, (("v", 32), ("s", 32))))
+W2_LOADS = (256, 256)
+W2_CHUNKS = ((0, 256, (("v", 160), ("g", 96))), (256, 256, (("v", 160), ("s", 96))))
+V_GATHER = 288
 
 
 def tile_picked_shuffle_mlp_silu_perm_l_kernel(tc, xT, w1, w2, offs, out):
@@ -31,24 +31,21 @@ def tile_picked_shuffle_mlp_silu_perm_l_kernel(tc, xT, w1, w2, offs, out):
         keep = ctx.enter_context(tc.tile_pool(name="keep", bufs=1))
         psum = ctx.enter_context(tc.psum_pool(name="psum", bufs=1))
 
+        def load(dram, widths, name):
+            raws = []
+            c0 = 0
+            for i, width in enumerate(widths):
+                raw = keep.tile([P, PACK, width], F32, name=f"{name}_raw{i}")
+                nc.sync.dma_start(raw[:], dram[:, c0 : c0 + width].rearrange("(p j) w -> p j w", j=PACK))
+                raws.append(raw)
+                c0 += width
+            return raws
+
         offsets = keep.tile([P, H // 16], U16, name="offsets")
-        x_raw = keep.tile([P, PACK, T], F32, name="x_raw")
-        nc.sync.dma_start(x_raw[:], xT.rearrange("(p j) t -> p j t", j=PACK))
-        w1_raw = []
-        c0 = 0
-        for i, width in enumerate(W1_PIECES):
-            raw = keep.tile([P, PACK, width], F32, name=f"w1_raw{i}")
-            nc.sync.dma_start(raw[:], w1[:, c0 : c0 + width].rearrange("(p j) w -> p j w", j=PACK))
-            w1_raw.append(raw)
-            c0 += width
+        x_raw = load(xT, (T,), "x")
+        w1_raw = load(w1, W1_LOADS, "w1")
         nc.sync.dma_start(offsets[:], offs)
-        w2_raw = []
-        c0 = 0
-        for i, width in enumerate(W2_PIECES):
-            raw = keep.tile([P, PACK, width], F32, name=f"w2_raw{i}")
-            nc.sync.dma_start(raw[:], w2[:, c0 : c0 + width].rearrange("(p j) w -> p j w", j=PACK))
-            w2_raw.append(raw)
-            c0 += width
+        w2_raw = load(w2, W2_LOADS, "w2")
 
         warm = keep.tile([P, 1], F32, name="warm")
         nc.vector.memset(warm[:], 0.0)
@@ -56,35 +53,48 @@ def tile_picked_shuffle_mlp_silu_perm_l_kernel(tc, xT, w1, w2, offs, out):
         ident = keep.tile([P, P], F32, name="ident")
         make_identity(nc, ident[:])
 
+        def chunk_codes(raws, loads, chunk, name, codes, scales):
+            c0, width, shares = chunk
+            first = 0
+            which = 0
+            while c0 >= first + loads[which]:
+                first += loads[which]
+                which += 1
+            src = raws[which][:].rearrange("p j w -> p w j")
+            grouped = keep.tile([P, width, PACK], BF16, name=f"{name}_grouped{c0}", align_bytes=64)
+            a = 0
+            for engine, share in shares:
+                dst = grouped[:, a : a + share, :]
+                part = src[:, c0 - first + a : c0 - first + a + share, :]
+                if engine == "v":
+                    nc.vector.tensor_copy(out=dst, in_=part)
+                elif engine == "s":
+                    nc.scalar.copy(out=dst, in_=part)
+                else:
+                    nc.gpsimd.tensor_scalar(
+                        out=dst, in0=part, scalar1=1.0, scalar2=0.0, op0=mybir.AluOpType.mult, op1=mybir.AluOpType.add
+                    )
+                a += share
+            quantize(grouped[:], codes[:, c0 : c0 + width], scales[:, c0 : c0 + width])
+
         def quantize(grouped, codes, scales):
             nc.vector.quantize_mx(
                 out=codes.bitcast(FP8X4), scales=scales, in_=grouped.rearrange("p w j -> p (w j)")
             )
 
-        def interleave(raw, grouped, width, vector_share):
-            src = raw[:].rearrange("p j w -> p w j")
-            if vector_share > 0:
-                nc.vector.tensor_copy(out=grouped[:, 0:vector_share, :], in_=src[:, 0:vector_share, :])
-            if vector_share < width:
-                nc.scalar.copy(out=grouped[:, vector_share:width, :], in_=src[:, vector_share:width, :])
-
-        x_grouped = keep.tile([P, T, PACK], BF16, name="x_grouped", align_bytes=64)
         x_codes = keep.tile([P, T], U32, name="x_codes", align_bytes=64)
         x_scales = keep.tile([P, T], U8, name="x_scales", align_bytes=64)
-        interleave(x_raw, x_grouped, T, T)
-        quantize(x_grouped[:], x_codes[:], x_scales[:])
+        chunk_codes(x_raw, (T,), (0, T, (("v", 128),)), "x", x_codes, x_scales)
 
         w1_codes = keep.tile([P, H], U32, name="w1_codes", align_bytes=64)
         w1_scales = keep.tile([P, H], U8, name="w1_scales", align_bytes=64)
         h = keep.tile([P, H], F32, name="h", align_bytes=64)
         h16 = keep.tile([P, H], BF16, name="h16", align_bytes=64)
-        c0 = 0
-        for i, width in enumerate(W1_PIECES):
+        for chunk in W1_CHUNKS:
+            c0, width, shares = chunk
             cols = slice(c0, c0 + width)
-            grouped = keep.tile([P, width, PACK], BF16, name=f"w1_grouped{i}", align_bytes=64)
-            interleave(w1_raw[i], grouped, width, W1_VECTOR[i])
-            quantize(grouped[:], w1_codes[:, cols], w1_scales[:, cols])
-            acc = psum.tile([P, width], F32, name=f"acc{i}")
+            chunk_codes(w1_raw, W1_LOADS, chunk, "w1", w1_codes, w1_scales)
+            acc = psum.tile([P, width], F32, name=f"acc{c0}")
             nc.tensor.matmul_mx(
                 out=acc[:],
                 lhsT=x_codes[:].bitcast(FP8X4),
@@ -97,7 +107,6 @@ def tile_picked_shuffle_mlp_silu_perm_l_kernel(tc, xT, w1, w2, offs, out):
             nc.scalar.activation(h[:, cols], acc[:], SILU)
             if V_GATHER < H:
                 nc.scalar.activation(h16[:, cols], acc[:], SILU)
-            c0 += width
 
         picked = keep.tile([P, H], BF16, name="picked", align_bytes=64)
         ordered = picked[:].rearrange("q (u p e) -> q p u e", u=2, e=2)
@@ -108,16 +117,6 @@ def tile_picked_shuffle_mlp_silu_perm_l_kernel(tc, xT, w1, w2, offs, out):
             nc.scalar.activation(
                 ordered[:, V_GATHER // PACK : P], h16[:].indirect(offsets[:, V_GATHER // 16 : H // 16]), COPY
             )
-
-        w2_codes = keep.tile([P, N], U32, name="w2_codes", align_bytes=64)
-        w2_scales = keep.tile([P, N], U8, name="w2_scales", align_bytes=64)
-        c0 = 0
-        for i, width in enumerate(W2_PIECES):
-            cols = slice(c0, c0 + width)
-            grouped = keep.tile([P, width, PACK], BF16, name=f"w2_grouped{i}", align_bytes=64)
-            interleave(w2_raw[i], grouped, width, W2_VECTOR[i])
-            quantize(grouped[:], w2_codes[:, cols], w2_scales[:, cols])
-            c0 += width
 
         turned = psum.tile([P, 2, T], F32, name="turned")
         words = picked[:].bitcast(F32)
@@ -131,6 +130,11 @@ def tile_picked_shuffle_mlp_silu_perm_l_kernel(tc, xT, w1, w2, offs, out):
         h_codes = keep.tile([P, T], U32, name="h_codes", align_bytes=64)
         h_scales = keep.tile([P, T], U8, name="h_scales", align_bytes=64)
         quantize(h_grouped[:], h_codes[:], h_scales[:])
+
+        w2_codes = keep.tile([P, N], U32, name="w2_codes", align_bytes=64)
+        w2_scales = keep.tile([P, N], U8, name="w2_scales", align_bytes=64)
+        for chunk in W2_CHUNKS:
+            chunk_codes(w2_raw, W2_LOADS, chunk, "w2", w2_codes, w2_scales)
 
         for half in range(2):
             acc2 = psum.tile([P, 2, T], F32, name=f"acc2_{half}")

@@ -23,6 +23,7 @@ W1_CHUNKS = ((0, 256, (("v", 176), ("s", 80))), (256, 64, (("v", 44), ("s", 20))
 W2_LOADS = (256, 256)
 W2_CHUNKS = ((0, 256, (("v", 160), ("g", 96))), (256, 256, (("v", 160), ("s", 96))))
 V_GATHER = 288
+BANKS = ("acc0", "acc256", "acc320", "acc2_3")
 
 
 def tile_picked_shuffle_mlp_silu_perm_l_kernel(tc, xT, w1, w2, offs, out):
@@ -82,6 +83,14 @@ def tile_picked_shuffle_mlp_silu_perm_l_kernel(tc, xT, w1, w2, offs, out):
                 out=codes.bitcast(FP8X4), scales=scales, in_=grouped.rearrange("p w j -> p (w j)")
             )
 
+        junk = psum.tile([P, 4, P], F32, name="junk")
+
+        def warm_up(raw, c):
+            for j in range(PACK):
+                nc.tensor.transpose(junk[:, j, :], raw[:, j, c : c + P], ident[:])
+
+        warm_up(w1_raw[0], 0)
+        warm_up(w1_raw[0], P)
         x_codes = keep.tile([P, T], U32, name="x_codes", align_bytes=64)
         x_scales = keep.tile([P, T], U8, name="x_scales", align_bytes=64)
         chunk_codes(x_raw, (T,), (0, T, (("v", 128),)), "x", x_codes, x_scales)
@@ -108,6 +117,8 @@ def tile_picked_shuffle_mlp_silu_perm_l_kernel(tc, xT, w1, w2, offs, out):
             if V_GATHER < H:
                 nc.scalar.activation(h16[:, cols], acc[:], SILU)
 
+        warm_up(w2_raw[0], 0)
+        warm_up(w2_raw[0], P)
         picked = keep.tile([P, H], BF16, name="picked", align_bytes=64)
         ordered = picked[:].rearrange("q (u p e) -> q p u e", u=2, e=2)
         nc.vector.tensor_copy(
@@ -136,24 +147,25 @@ def tile_picked_shuffle_mlp_silu_perm_l_kernel(tc, xT, w1, w2, offs, out):
         for chunk in W2_CHUNKS:
             chunk_codes(w2_raw, W2_LOADS, chunk, "w2", w2_codes, w2_scales)
 
-        for half in range(2):
-            acc2 = psum.tile([P, 2, T], F32, name=f"acc2_{half}")
-            for b in range(2):
-                m = slice((2 * half + b) * P, (2 * half + b + 1) * P)
-                nc.tensor.matmul_mx(
-                    out=acc2[:, b, :],
-                    lhsT=w2_codes[:, m].bitcast(FP8X4),
-                    lhsT_scale=w2_scales[:, m],
-                    rhs=h_codes[:].bitcast(FP8X4),
-                    rhs_scale=h_scales[:],
-                    start=True,
-                    stop=True,
-                )
-            result = keep.tile([P, 2, T], F32, name=f"result{half}")
-            rows = out[2 * P * half : 2 * P * (half + 1), :].rearrange("(b p) t -> p b t", p=P)
-            if half == 0:
-                nc.vector.tensor_copy(out=result[:], in_=acc2[:])
-                nc.sync.dma_start(rows, result[:])
+        blocks = N // P
+        results = keep.tile([P, blocks, T], F32, name="results")
+        for b in range(blocks):
+            m = slice(b * P, (b + 1) * P)
+            acc2 = psum.tile([P, T], F32, name=f"acc2_{b}", tag=BANKS[b])
+            nc.tensor.matmul_mx(
+                out=acc2[:],
+                lhsT=w2_codes[:, m].bitcast(FP8X4),
+                lhsT_scale=w2_scales[:, m],
+                rhs=h_codes[:].bitcast(FP8X4),
+                rhs_scale=h_scales[:],
+                start=True,
+                stop=True,
+            )
+            if b % 2 == 0:
+                nc.vector.tensor_copy(out=results[:, b, :], in_=acc2[:])
             else:
-                nc.scalar.copy(out=result[:], in_=acc2[:])
-                nc.scalar.dma_start(rows, result[:])
+                nc.scalar.copy(out=results[:, b, :], in_=acc2[:])
+        rows = out.rearrange("(b p) t -> p b t", p=P)
+        nc.sync.dma_start(rows[:, 0:2, :], results[:, 0:2, :])
+        nc.sync.dma_start(rows[:, 2:3, :], results[:, 2:3, :])
+        nc.scalar.dma_start(rows[:, 3:4, :], results[:, 3:4, :])

@@ -21,7 +21,7 @@ PACK = 4
 W1_LOADS = (320, 192)
 W1_CHUNKS = ((0, 256, (("v", 176), ("s", 80))), (256, 64, (("v", 44), ("s", 20))), (320, 128, (("v", 80), ("s", 48))), (448, 64, (("v", 32), ("s", 32))))
 W2_LOADS = (256, 256)
-W2_CHUNKS = ((0, 256, (("v", 160), ("g", 96))), (256, 256, (("v", 160), ("s", 96))))
+W2_CHUNKS = ((0, 256, (("g", 128), ("g", 128))), (256, 256, (("v", 160), ("s", 96))))
 V_GATHER = 288
 BANKS = ("acc0", "acc256", "acc320", "acc2_3")
 
@@ -89,8 +89,6 @@ def tile_picked_shuffle_mlp_silu_perm_l_kernel(tc, xT, w1, w2, offs, out):
             for j in range(PACK):
                 nc.tensor.transpose(junk[:, j, :], raw[:, j, c : c + P], ident[:])
 
-        warm_up(w1_raw[0], 0)
-        warm_up(w1_raw[0], P)
         x_codes = keep.tile([P, T], U32, name="x_codes", align_bytes=64)
         x_scales = keep.tile([P, T], U8, name="x_scales", align_bytes=64)
         chunk_codes(x_raw, (T,), (0, T, (("v", 128),)), "x", x_codes, x_scales)
@@ -99,11 +97,13 @@ def tile_picked_shuffle_mlp_silu_perm_l_kernel(tc, xT, w1, w2, offs, out):
         w1_scales = keep.tile([P, H], U8, name="w1_scales", align_bytes=64)
         h = keep.tile([P, H], F32, name="h", align_bytes=64)
         h16 = keep.tile([P, H], BF16, name="h16", align_bytes=64)
+        accs = []
         for chunk in W1_CHUNKS:
             c0, width, shares = chunk
             cols = slice(c0, c0 + width)
             chunk_codes(w1_raw, W1_LOADS, chunk, "w1", w1_codes, w1_scales)
             acc = psum.tile([P, width], F32, name=f"acc{c0}")
+            accs.append((cols, acc))
             nc.tensor.matmul_mx(
                 out=acc[:],
                 lhsT=x_codes[:].bitcast(FP8X4),
@@ -114,9 +114,9 @@ def tile_picked_shuffle_mlp_silu_perm_l_kernel(tc, xT, w1, w2, offs, out):
                 stop=True,
             )
             nc.scalar.activation(h[:, cols], acc[:], SILU)
-            if V_GATHER < H:
-                nc.scalar.activation(h16[:, cols], acc[:], SILU)
 
+        for cols, acc in accs:
+            nc.scalar.activation(h16[:, cols], acc[:], SILU)
         warm_up(w2_raw[0], 0)
         warm_up(w2_raw[0], P)
         picked = keep.tile([P, H], BF16, name="picked", align_bytes=64)

from contextlib import ExitStack

import concourse.mybir as mybir
from concourse.masks import make_identity

K, T, H, N = 512, 128, 512, 512
FLOPS = 2 * T * H * (K + N)

F32 = mybir.dt.float32
BF16 = mybir.dt.bfloat16
U32 = mybir.dt.uint32
U16 = mybir.dt.uint16
U8 = mybir.dt.uint8
FP8X4 = mybir.dt.float8_e4m3fn_x4
SILU = mybir.ActivationFunctionType.Silu
COPY = mybir.ActivationFunctionType.Copy

P = 128
PACK = 4

W1_LOADS = (320, 192)
W1_CHUNKS = ((0, 256, (("v", 176), ("s", 80))), (256, 64, (("v", 44), ("s", 20))), (320, 128, (("v", 80), ("s", 48))), (448, 64, (("v", 32), ("s", 32))))
W2_LOADS = (256, 256)
W2_CHUNKS = ((0, 256, (("g", 128), ("g", 128))), (256, 256, (("v", 160), ("s", 96))))
V_GATHER = 288
BANKS = ("acc0", "acc256", "acc320", "acc2_3")


def tile_picked_shuffle_mlp_silu_perm_l_kernel(tc, xT, w1, w2, offs, out):
    nc = tc.nc
    with ExitStack() as ctx:
        keep = ctx.enter_context(tc.tile_pool(name="keep", bufs=1))
        psum = ctx.enter_context(tc.psum_pool(name="psum", bufs=1))

        def load(dram, widths, name):
            raws = []
            c0 = 0
            for i, width in enumerate(widths):
                raw = keep.tile([P, PACK, width], F32, name=f"{name}_raw{i}")
                nc.sync.dma_start(raw[:], dram[:, c0 : c0 + width].rearrange("(p j) w -> p j w", j=PACK))
                raws.append(raw)
                c0 += width
            return raws

        offsets = keep.tile([P, H // 16], U16, name="offsets")
        x_raw = load(xT, (T,), "x")
        w1_raw = load(w1, W1_LOADS, "w1")
        nc.sync.dma_start(offsets[:], offs)
        w2_raw = load(w2, W2_LOADS, "w2")

        warm = keep.tile([P, 1], F32, name="warm")
        nc.vector.memset(warm[:], 0.0)
        nc.scalar.activation(warm[:], warm[:], SILU)
        ident = keep.tile([P, P], F32, name="ident")
        make_identity(nc, ident[:])

        def chunk_codes(raws, loads, chunk, name, codes, scales):
            c0, width, shares = chunk
            first = 0
            which = 0
            while c0 >= first + loads[which]:
                first += loads[which]
                which += 1
            src = raws[which][:].rearrange("p j w -> p w j")
            grouped = keep.tile([P, width, PACK], BF16, name=f"{name}_grouped{c0}", align_bytes=64)
            a = 0
            for engine, share in shares:
                dst = grouped[:, a : a + share, :]
                part = src[:, c0 - first + a : c0 - first + a + share, :]
                if engine == "v":
                    nc.vector.tensor_copy(out=dst, in_=part)
                elif engine == "s":
                    nc.scalar.copy(out=dst, in_=part)
                else:
                    nc.gpsimd.tensor_scalar(
                        out=dst, in0=part, scalar1=1.0, scalar2=0.0, op0=mybir.AluOpType.mult, op1=mybir.AluOpType.add
                    )
                a += share
            quantize(grouped[:], codes[:, c0 : c0 + width], scales[:, c0 : c0 + width])

        def quantize(grouped, codes, scales):
            nc.vector.quantize_mx(
                out=codes.bitcast(FP8X4), scales=scales, in_=grouped.rearrange("p w j -> p (w j)")
            )

        junk = psum.tile([P, 4, P], F32, name="junk")

        def warm_up(raw, c):
            for j in range(PACK):
                nc.tensor.transpose(junk[:, j, :], raw[:, j, c : c + P], ident[:])

        x_codes = keep.tile([P, T], U32, name="x_codes", align_bytes=64)
        x_scales = keep.tile([P, T], U8, name="x_scales", align_bytes=64)
        chunk_codes(x_raw, (T,), (0, T, (("v", 128),)), "x", x_codes, x_scales)

        w1_codes = keep.tile([P, H], U32, name="w1_codes", align_bytes=64)
        w1_scales = keep.tile([P, H], U8, name="w1_scales", align_bytes=64)
        h = keep.tile([P, H], F32, name="h", align_bytes=64)
        h16 = keep.tile([P, H], BF16, name="h16", align_bytes=64)
        accs = []
        for chunk in W1_CHUNKS:
            c0, width, shares = chunk
            cols = slice(c0, c0 + width)
            chunk_codes(w1_raw, W1_LOADS, chunk, "w1", w1_codes, w1_scales)
            acc = psum.tile([P, width], F32, name=f"acc{c0}")
            accs.append((cols, acc))
            nc.tensor.matmul_mx(
                out=acc[:],
                lhsT=x_codes[:].bitcast(FP8X4),
                lhsT_scale=x_scales[:],
                rhs=w1_codes[:, cols].bitcast(FP8X4),
                rhs_scale=w1_scales[:, cols],
                start=True,
                stop=True,
            )
            nc.scalar.activation(h[:, cols], acc[:], SILU)

        for cols, acc in accs:
            nc.scalar.activation(h16[:, cols], acc[:], SILU)
        warm_up(w2_raw[0], 0)
        warm_up(w2_raw[0], P)
        picked = keep.tile([P, H], BF16, name="picked", align_bytes=64)
        ordered = picked[:].rearrange("q (u p e) -> q p u e", u=2, e=2)
        nc.vector.tensor_copy(
            ordered[:, 0 : V_GATHER // PACK], h[:].indirect(offsets[:, 0 : V_GATHER // 16])
        )
        if V_GATHER < H:
            nc.scalar.activation(
                ordered[:, V_GATHER // PACK : P], h16[:].indirect(offsets[:, V_GATHER // 16 : H // 16]), COPY
            )

        turned = psum.tile([P, 2, T], F32, name="turned")
        words = picked[:].bitcast(F32)
        for u in range(2):
            nc.tensor.transpose(turned[:, u, :], words[:, u * P : (u + 1) * P], ident[:])
        h_grouped = keep.tile([P, T, PACK], BF16, name="h_grouped", align_bytes=64)
        nc.scalar.copy(
            out=h_grouped[:].rearrange("p t j -> p (t j)").bitcast(F32).rearrange("p (t u) -> p t u", u=2),
            in_=turned[:].rearrange("p u t -> p t u"),
        )
        h_codes = keep.tile([P, T], U32, name="h_codes", align_bytes=64)
        h_scales = keep.tile([P, T], U8, name="h_scales", align_bytes=64)
        quantize(h_grouped[:], h_codes[:], h_scales[:])

        w2_codes = keep.tile([P, N], U32, name="w2_codes", align_bytes=64)
        w2_scales = keep.tile([P, N], U8, name="w2_scales", align_bytes=64)
        for chunk in W2_CHUNKS:
            chunk_codes(w2_raw, W2_LOADS, chunk, "w2", w2_codes, w2_scales)

        blocks = N // P
        results = keep.tile([P, blocks, T], F32, name="results")
        for b in range(blocks):
            m = slice(b * P, (b + 1) * P)
            acc2 = psum.tile([P, T], F32, name=f"acc2_{b}", tag=BANKS[b])
            nc.tensor.matmul_mx(
                out=acc2[:],
                lhsT=w2_codes[:, m].bitcast(FP8X4),
                lhsT_scale=w2_scales[:, m],
                rhs=h_codes[:].bitcast(FP8X4),
                rhs_scale=h_scales[:],
                start=True,
                stop=True,
            )
            if b % 2 == 0:
                nc.vector.tensor_copy(out=results[:, b, :], in_=acc2[:])
            else:
                nc.scalar.copy(out=results[:, b, :], in_=acc2[:])
        rows = out.rearrange("(b p) t -> p b t", p=P)
        nc.sync.dma_start(rows[:, 0:2, :], results[:, 0:2, :])
        nc.sync.dma_start(rows[:, 2:3, :], results[:, 2:3, :])
        nc.scalar.dma_start(rows[:, 3:4, :], results[:, 3:4, :])
